import numpy as np
import ml_dtypes


def mxq(x, axis, fmt="e4m3"):
    dtype, down = {"e4m3": (ml_dtypes.float8_e4m3fn, 7), "e5m2": (ml_dtypes.float8_e5m2, 14)}[fmt]
    v = np.moveaxis(np.asarray(x, np.float32).astype(ml_dtypes.bfloat16).astype(np.float64), axis, -1)
    blocks = v.reshape(v.shape[:-1] + (-1, 32))
    amax = np.abs(blocks).max(-1, keepdims=True)
    byte = np.maximum(np.where(amax > 0, np.frexp(amax)[1] - 1 + 127, 0) - down, 1)
    scale = np.exp2(byte - 127.0)
    codes = (blocks / scale).astype(np.float32).astype(dtype).astype(np.float64)
    return np.moveaxis((codes * scale).reshape(v.shape), -1, axis)


WIDE = False


def mx_kscale(k):
    if not WIDE:
        return np.ones(k)
    levels = np.array([10, -10, 5, -5, 0])
    if k % 512:
        return np.exp2(np.random.permutation(np.resize(levels, k // 32))).repeat(32)
    a = np.empty((k // 512, 16))
    for p in range(k // 512):
        a[p, :8] = np.random.permutation(np.resize(levels, 8))
        for g in range(8):
            far = levels[np.abs(levels - a[p, g]) >= 10]
            a[p, g + 8] = far[np.random.randint(len(far))]
    return np.exp2(a.ravel()).repeat(32)


def f64(x):
    return np.asarray(x).astype(np.float64)


def striped(idx):
    return np.tile(idx.reshape(-1, 16).T, (8, 1)).astype(np.uint16)


def unstriped(offs):
    return offs[:16].T.reshape(-1).astype(np.int64)


def pack_weight(w):
    k, n = w.shape
    w = f64(np.asarray(w, np.float32).astype(ml_dtypes.bfloat16)).reshape(k // 32, 32, n)
    amax = np.abs(w).max(1)
    byte = np.clip(np.where(amax > 0, np.frexp(amax)[1] - 1 + 127 - 7, 1), 1, 254)
    scaled = (w * np.exp2(127.0 - byte)[:, None, :]).reshape(k, n).astype(np.float32)
    words = np.ascontiguousarray(scaled.reshape(k // 512, 128, 4, n).transpose(0, 1, 3, 2)).astype(ml_dtypes.float8_e4m3fn).view(np.uint8)
    return words, np.ascontiguousarray(byte.astype(np.uint8).reshape(k // 512, 16, n))


def unpack_weight(words, scales):
    g, p, n, _ = words.shape
    vals = np.ascontiguousarray(words).view(ml_dtypes.float8_e4m3fn).astype(np.float64) * np.repeat(np.exp2(scales.astype(np.float64) - 127.0), 8, axis=1)[..., None]
    return vals.transpose(0, 1, 3, 2).reshape(g * 512, n)


K, T, S, H, W = 512, 2048, 512, 512, 384


def setup_inputs():
    n = np.random.standard_normal
    s = mx_kscale(K)[:, None]
    u = mx_kscale(S)
    packed_xT = pack_weight(n((K, T)) * s)
    return {
        "x_words": packed_xT[0],
        "x_scales": packed_xT[1],
        "wa": (n((K, H)) / np.sqrt(K) / s).astype(np.float32),
        "wb": (n((K, H)) / np.sqrt(K) / s).astype(np.float32),
        "gt": (np.random.uniform(0.5, 1.5, (S, 1)) * u[:, None]).astype(np.float32),
        "gi": (np.random.uniform(0.5, 1.5, (S, 1)) / u[:, None]).astype(np.float32),
        "offs": striped(np.random.permutation(T)[:S]),
        "two": striped(np.random.permutation(T)[:S]),
        "n1": striped(np.random.permutation(H)),
        "n2": striped(np.random.permutation(H)),
        "n3": striped(np.random.permutation(H)[:W]),
        "n4": striped(np.random.permutation(H)[:W]),
    }


def reference(x_words, x_scales, wa, wb, gt, gi, offs, two, n1, n2, n3, n4):
    xq = unpack_weight(x_words, x_scales)[:, unstriped(offs)]
    a = xq.T @ mxq(f64(wa), 0, "e4m3")
    x_two = unpack_weight(x_words, x_scales)[:, unstriped(two)]
    b = x_two.T @ mxq(f64(wb), 0, "e4m3")
    z = f64(gt) * (a * (np.tanh(b[:, unstriped(n1)] - b[:, unstriped(n2)])))
    z2 = f64(gi) * b
    cv = 0.0625 * ((mxq(z, 0, "e4m3").T @ mxq(z2, 0, "e4m3")))
    old = cv[:, unstriped(n3)]
    pa = cv[:, unstriped(n4)]
    ra = old - np.tanh(pa)
    out = cv.copy()
    out[:, unstriped(n3)] = ra
    return out

@@ -1,0 +1,209 @@
+from contextlib import ExitStack
+
+import concourse.mybir as mybir
+from concourse.masks import make_identity
+
+K, T, S, H, W = 512, 2048, 512, 512, 384
+FLOPS = 2 * K * S * H * 2 + 2 * S * H * H
+
+F32 = mybir.dt.float32
+BF16 = mybir.dt.bfloat16
+I32 = mybir.dt.int32
+U32 = mybir.dt.uint32
+U16 = mybir.dt.uint16
+U8 = mybir.dt.uint8
+FP8X4 = mybir.dt.float8_e4m3fn_x4
+MULT = mybir.AluOpType.mult
+ADD = mybir.AluOpType.add
+SUB = mybir.AluOpType.subtract
+COPY = mybir.ActivationFunctionType.Copy
+TANH = mybir.ActivationFunctionType.Tanh
+
+P = 128
+PACK = 4
+RUN = 8
+BLK = 128
+NBLK = H // BLK
+LIST_COLS = BLK // 16
+WB_SCALAR_COLS = 320
+
+
+def interleave(copy, grouped, planes):
+    copy(
+        grouped.rearrange("p (c i) t -> p c t i", i=4),
+        planes.rearrange("p t (c i) -> p c t i", i=4),
+    )
+
+
+def tile_picked_momtjointbktanh_none_p_kernel(
+    tc, x_words, x_scales, wa, wb, gt, gi, offs, two, n1, n2, n3, n4, out
+):
+    nc = tc.nc
+    with ExitStack() as ctx:
+        keep = ctx.enter_context(tc.tile_pool(name="keep", bufs=1))
+        psum = ctx.enter_context(tc.psum_pool(name="psum", bufs=4))
+
+        def sbuf(name, shape, dtype):
+            return keep.tile(shape, dtype, name=name, align_bytes=64)
+
+        def load_list(name, src):
+            dst = sbuf(name, list(src.shape), U16)
+            nc.sync.dma_start(dst[:], src)
+            return dst
+
+        def load_weight(name, w):
+            dst = keep.tile([P, PACK, H], F32, name=name, tag="w_raw", align_bytes=64)
+            nc.sync.dma_start(dst[:], w.rearrange("(p j) n -> p j n", j=PACK))
+            return dst
+
+        def quantize(name, grouped, width):
+            codes = sbuf(name + "_codes", [P, width], U32)
+            scales = sbuf(name + "_scales", [P, width], U8)
+            nc.vector.quantize_mx(
+                out=codes[:].bitcast(FP8X4), scales=scales[:], in_=grouped[:].rearrange("p n t -> p (n t)")
+            )
+            return codes, scales
+
+        def matmul(dst, lhs_codes, lhs_scales, rhs_codes, rhs_scales):
+            nc.tensor.matmul_mx(
+                out=dst,
+                lhsT=lhs_codes.bitcast(FP8X4),
+                lhsT_scale=lhs_scales,
+                rhs=rhs_codes.bitcast(FP8X4),
+                rhs_scale=rhs_scales,
+                start=True,
+                stop=True,
+            )
+
+        scale_table = sbuf("scale_table", [P, T], U8)
+        nc.gpsimd.memset(scale_table[:].bitcast(I32), 0)
+        for q in range(4):
+            nc.sync.dma_start(
+                scale_table[32 * q : 32 * q + 4, :].bitcast(I32), x_scales[0, 4 * q : 4 * q + 4, :].bitcast(I32)
+            )
+        two_list = load_list("two_list", two)
+        offs_list = load_list("offs_list", offs)
+        wb_raw = load_weight("wb_raw", wb)
+        word_table = sbuf("word_table", [P, T], I32)
+        nc.sync.dma_start(word_table[:], x_words[0].rearrange("p n t -> p (n t)").bitcast(I32))
+        gate_rows = sbuf("gate_rows", [P, P], F32)
+        nc.gpsimd.memset(gate_rows[:], 0.0)
+        for row, gate in ((0, gt), (PACK, gi)):
+            nc.sync.dma_start(
+                gate_rows[row : row + PACK, :].rearrange("t (g r) -> t g r", r=RUN),
+                gate.rearrange("(g t r) o -> t g (r o)", t=PACK, r=RUN),
+            )
+        identity = sbuf("identity", [P, P], F32)
+        make_identity(nc, identity[:])
+        n1_list = load_list("n1_list", n1)
+        n2_list = load_list("n2_list", n2)
+        n3_list = load_list("n3_list", n3)
+        n4_list = load_list("n4_list", n4)
+
+        def pick_scales(name, entries):
+            picked = sbuf(name + "_picked", [P, S], U8)
+            nc.vector.tensor_copy(picked[:], scale_table[:].indirect(entries[:]))
+            dealt = sbuf(name + "_dealt", [P, PACK, P], U8)
+            nc.vector.tensor_copy(
+                dealt[:].bitcast(I32).rearrange("p t (g w) -> p g t w", w=RUN // 4),
+                picked[:].bitcast(I32).rearrange("p (g t w) -> p g t w", t=PACK, w=RUN // 4),
+            )
+            return dealt
+
+        def pick_words(name, entries):
+            dealt = sbuf(name, [P, PACK, P], U32)
+            nc.vector.tensor_copy(
+                dealt[:].rearrange("p t (g r) -> p g t r", r=RUN), word_table[:].bitcast(U32).indirect(entries[:])
+            )
+            return dealt
+
+        xb_scales = pick_scales("xb_scales", two_list)
+        xa_scales = pick_scales("xa_scales", offs_list)
+
+        wb_grouped = sbuf("wb_grouped", [P, H, PACK], BF16)
+        interleave(nc.scalar.copy, wb_grouped[:, :WB_SCALAR_COLS, :], wb_raw[:, :, :WB_SCALAR_COLS])
+        interleave(nc.vector.tensor_copy, wb_grouped[:, WB_SCALAR_COLS:, :], wb_raw[:, :, WB_SCALAR_COLS:])
+        wb_codes, wb_scales = quantize("wb", wb_grouped, H)
+        wa_raw = load_weight("wa_raw", wa)
+        xb_words = pick_words("xb_words", two_list)
+
+        b_bank = [psum.tile([P, H], F32, name="b_bank%d" % t, tag="bcv") for t in range(PACK)]
+        for t in range(PACK):
+            matmul(b_bank[t][:], xb_words[:, t, :], xb_scales[:, t, :], wb_codes[:], wb_scales[:])
+        gate_bank = psum.tile([P, P], F32, name="gate_bank", tag="a")
+        nc.tensor.transpose(gate_bank[:], gate_rows[:], identity[:])
+        gates = sbuf("gates", [P, 2 * PACK], F32)
+        nc.scalar.copy(gates[:], gate_bank[:, 0 : 2 * PACK])
+        xa_words = pick_words("xa_words", offs_list)
+
+        b_rows = [sbuf("b_rows%d" % t, [P, H], F32) for t in range(PACK)]
+        z2_planes = sbuf("z2_planes", [P, PACK, H], BF16)
+        for t in range(PACK):
+            nc.scalar.copy(b_rows[t][:], b_bank[t][:])
+            nc.vector.tensor_scalar(z2_planes[:, t, :], b_rows[t][:], gates[:, PACK + t : PACK + t + 1], None, MULT)
+
+        a_bank, tanh_d, cv_bank, cv_rows, ra = {}, {}, {}, {}, {}
+        z2_mx = []
+
+        def project_a(ib):
+            grouped = sbuf("wa_grouped%d" % ib, [P, BLK, PACK], BF16)
+            interleave(nc.vector.tensor_copy, grouped[:], wa_raw[:, :, ib * BLK : (ib + 1) * BLK])
+            codes, scales = quantize("wa%d" % ib, grouped, BLK)
+            a_bank[ib] = psum.tile([P, PACK, BLK], F32, name="a_bank%d" % ib, tag="a")
+            for t in range(PACK):
+                matmul(a_bank[ib][:, t, :], xa_words[:, t, :], xa_scales[:, t, :], codes[:], scales[:])
+
+        def fetch_b(ib):
+            cols = slice(ib * LIST_COLS, (ib + 1) * LIST_COLS)
+            first = sbuf("b_n1_%d" % ib, [P, PACK, BLK], F32)
+            diff = sbuf("diff%d" % ib, [P, PACK, BLK], F32)
+            for t in range(PACK):
+                nc.scalar.activation(first[:, t, :], b_rows[t][:].indirect(n1_list[:, cols]), COPY)
+            for t in range(PACK):
+                nc.vector.tensor_tensor(diff[:, t, :], b_rows[t][:].indirect(n2_list[:, cols]), first[:, t, :], SUB)
+            tanh_d[ib] = sbuf("tanh_d%d" % ib, [P, PACK, BLK], F32)
+            nc.scalar.activation(tanh_d[ib][:], diff[:], TANH, scale=-1.0)
+
+        def make_z2():
+            grouped = sbuf("z2_grouped", [P, H, PACK], BF16)
+            interleave(nc.vector.tensor_copy, grouped[:], z2_planes[:])
+            z2_mx.extend(quantize("z2", grouped, H))
+
+        def moments(ib):
+            planes = sbuf("z_planes%d" % ib, [P, PACK, BLK], BF16)
+            for t in range(PACK):
+                nc.vector.scalar_tensor_tensor(
+                    planes[:, t, :], tanh_d[ib][:, t, :], gates[:, t : t + 1], a_bank[ib][:, t, :], MULT, MULT
+                )
+            grouped = sbuf("z_grouped%d" % ib, [P, BLK, PACK], BF16)
+            interleave(nc.vector.tensor_copy, grouped[:], planes[:])
+            codes, scales = quantize("z_block%d" % ib, grouped, BLK)
+            cv_bank[ib] = psum.tile([P, H], F32, name="cv_bank%d" % ib, tag="bcv")
+            matmul(cv_bank[ib][:], codes[:], scales[:], z2_mx[0][:], z2_mx[1][:])
+
+        def fetch_cv(ib):
+            cv_rows[ib] = sbuf("cv_rows%d" % ib, [P, H], F32)
+            nc.vector.tensor_scalar(cv_rows[ib][:], cv_bank[ib][:], 0.0625, None, MULT)
+            neg_tanh = sbuf("neg_tanh%d" % ib, [P, H], F32)
+            nc.scalar.activation(neg_tanh[:], cv_rows[ib][:], TANH, scale=-1.0)
+            old = sbuf("old%d" % ib, [P, W], F32)
+            nc.scalar.activation(old[:], cv_rows[ib][:].indirect(n3_list[:]), COPY)
+            ra[ib] = sbuf("ra%d" % ib, [P, W], F32)
+            nc.vector.tensor_tensor(ra[ib][:], neg_tanh[:].indirect(n4_list[:]), old[:], ADD)
+
+        def put_back(ib):
+            nc.scalar.activation(cv_rows[ib][:].indirect(n3_list[:]), ra[ib][:], COPY)
+            nc.sync.dma_start(out[ib * BLK : (ib + 1) * BLK, :], cv_rows[ib][:])
+
+        project_a(0)
+        fetch_b(0)
+        make_z2()
+        for ib in range(NBLK + 1):
+            if ib + 1 < NBLK:
+                project_a(ib + 1)
+                fetch_b(ib + 1)
+            if ib < NBLK:
+                moments(ib)
+                fetch_cv(ib)
+            if ib > 0:
+                put_back(ib - 1)

@@ -22,10 +22,10 @@ TANH = mybir.ActivationFunctionType.Tanh
 P = 128
 PACK = 4
 RUN = 8
-BLK = 128
-NBLK = H // BLK
-LIST_COLS = BLK // 16
-WB_SCALAR_COLS = 320
+HALF = H // 2
+LIST_COLS = HALF // 16
+WB_SCALAR_COLS = (HALF, 160)
+Z2_SCALAR_COLS = 176
 
 
 def interleave(copy, grouped, planes):
@@ -43,21 +43,21 @@ def tile_picked_momtjointbktanh_none_p_kernel(
         keep = ctx.enter_context(tc.tile_pool(name="keep", bufs=1))
         psum = ctx.enter_context(tc.psum_pool(name="psum", bufs=4))
 
-        def sbuf(name, shape, dtype):
-            return keep.tile(shape, dtype, name=name, align_bytes=64)
+        def sbuf(name, shape, dtype, tag=""):
+            return keep.tile(shape, dtype, name=name, tag=tag, align_bytes=64)
 
         def load_list(name, src):
             dst = sbuf(name, list(src.shape), U16)
             nc.sync.dma_start(dst[:], src)
             return dst
 
-        def load_weight(name, w):
-            dst = keep.tile([P, PACK, H], F32, name=name, tag="w_raw", align_bytes=64)
-            nc.sync.dma_start(dst[:], w.rearrange("(p j) n -> p j n", j=PACK))
+        def load_weight_half(name, w, h):
+            dst = sbuf("%s%d" % (name, h), [P, PACK, HALF], F32)
+            nc.sync.dma_start(dst[:], w.rearrange("(p j) n -> p j n", j=PACK)[:, :, h * HALF : (h + 1) * HALF])
             return dst
 
-        def quantize(name, grouped, width):
-            codes = sbuf(name + "_codes", [P, width], U32)
+        def quantize(name, grouped, width, tag=""):
+            codes = sbuf(name + "_codes", [P, width], U32, tag)
             scales = sbuf(name + "_scales", [P, width], U8)
             nc.vector.quantize_mx(
                 out=codes[:].bitcast(FP8X4), scales=scales[:], in_=grouped[:].rearrange("p n t -> p (n t)")
@@ -83,9 +83,9 @@ def tile_picked_momtjointbktanh_none_p_kernel(
             )
         two_list = load_list("two_list", two)
         offs_list = load_list("offs_list", offs)
-        wb_raw = load_weight("wb_raw", wb)
         word_table = sbuf("word_table", [P, T], I32)
         nc.sync.dma_start(word_table[:], x_words[0].rearrange("p n t -> p (n t)").bitcast(I32))
+        wb_raw = [load_weight_half("wb_raw", wb, h) for h in range(2)]
         gate_rows = sbuf("gate_rows", [P, P], F32)
         nc.gpsimd.memset(gate_rows[:], 0.0)
         for row, gate in ((0, gt), (PACK, gi)):
@@ -97,6 +97,7 @@ def tile_picked_momtjointbktanh_none_p_kernel(
         make_identity(nc, identity[:])
         n1_list = load_list("n1_list", n1)
         n2_list = load_list("n2_list", n2)
+        wa_raw = [load_weight_half("wa_raw", wa, h) for h in range(2)]
         n3_list = load_list("n3_list", n3)
         n4_list = load_list("n4_list", n4)
 
@@ -110,8 +111,8 @@ def tile_picked_momtjointbktanh_none_p_kernel(
             )
             return dealt
 
-        def pick_words(name, entries):
-            dealt = sbuf(name, [P, PACK, P], U32)
+        def pick_words(name, entries, tag=""):
+            dealt = sbuf(name, [P, PACK, P], U32, tag)
             nc.vector.tensor_copy(
                 dealt[:].rearrange("p t (g r) -> p g t r", r=RUN), word_table[:].bitcast(U32).indirect(entries[:])
             )
@@ -119,91 +120,135 @@ def tile_picked_momtjointbktanh_none_p_kernel(
 
         xb_scales = pick_scales("xb_scales", two_list)
         xa_scales = pick_scales("xa_scales", offs_list)
-
-        wb_grouped = sbuf("wb_grouped", [P, H, PACK], BF16)
-        interleave(nc.scalar.copy, wb_grouped[:, :WB_SCALAR_COLS, :], wb_raw[:, :, :WB_SCALAR_COLS])
-        interleave(nc.vector.tensor_copy, wb_grouped[:, WB_SCALAR_COLS:, :], wb_raw[:, :, WB_SCALAR_COLS:])
-        wb_codes, wb_scales = quantize("wb", wb_grouped, H)
-        wa_raw = load_weight("wa_raw", wa)
         xb_words = pick_words("xb_words", two_list)
 
         b_bank = [psum.tile([P, H], F32, name="b_bank%d" % t, tag="bcv") for t in range(PACK)]
-        for t in range(PACK):
-            matmul(b_bank[t][:], xb_words[:, t, :], xb_scales[:, t, :], wb_codes[:], wb_scales[:])
+        for h in range(2):
+            cut = WB_SCALAR_COLS[h]
+            grouped = sbuf("wb_grouped%d" % h, [P, HALF, PACK], BF16)
+            interleave(nc.scalar.copy, grouped[:, :cut, :], wb_raw[h][:, :, :cut])
+            if cut < HALF:
+                interleave(nc.vector.tensor_copy, grouped[:, cut:, :], wb_raw[h][:, :, cut:])
+            codes, scales = quantize("wb%d" % h, grouped, HALF)
+            for t in range(PACK):
+                matmul(b_bank[t][:, h * HALF : (h + 1) * HALF], xb_words[:, t, :], xb_scales[:, t, :], codes[:], scales[:])
+
+        xa_words = pick_words("xa_words", offs_list, "wb_grouped1")
         gate_bank = psum.tile([P, P], F32, name="gate_bank", tag="a")
         nc.tensor.transpose(gate_bank[:], gate_rows[:], identity[:])
         gates = sbuf("gates", [P, 2 * PACK], F32)
         nc.scalar.copy(gates[:], gate_bank[:, 0 : 2 * PACK])
-        xa_words = pick_words("xa_words", offs_list)
 
+        wa_grouped, a_bank, b_n1, tanh_d, z_planes, z_grouped, cv_bank, cv_rows, neg_tanh, old, ra = ({} for i in range(11))
+
+        def round_wa(h, tag):
+            wa_grouped[h] = sbuf("wa_grouped%d" % h, [P, HALF, PACK], BF16, tag)
+            interleave(nc.scalar.copy, wa_grouped[h][:], wa_raw[h][:])
+
+        def project_a(h, tag=""):
+            codes, scales = quantize("wa%d" % h, wa_grouped[h], HALF, tag)
+            for u in range(2):
+                bank = psum.tile([P, 2, HALF], F32, name="a_bank%d%d" % (h, u), tag="a")
+                for e in range(2):
+                    t = 2 * u + e
+                    a_bank[h, t] = bank[:, e, :]
+                    matmul(a_bank[h, t], xa_words[:, t, :], xa_scales[:, t, :], codes[:], scales[:])
+
+        def entries(lst, h):
+            return lst[:, h * LIST_COLS : (h + 1) * LIST_COLS]
+
+        def fetch_n1(h, tag=""):
+            b_n1[h] = sbuf("b_n1_%d" % h, [P, PACK, HALF], F32, tag)
+            for t in range(PACK):
+                nc.scalar.activation(b_n1[h][:, t, :], b_rows[t][:].indirect(entries(n1_list, h)), COPY)
+
+        def fetch_n2(h, t, neg_diff):
+            nc.vector.tensor_tensor(neg_diff, b_rows[t][:].indirect(entries(n2_list, h)), b_n1[h][:, t, :], SUB)
+            tanh_d[h, t] = sbuf("tanh_d%d%d" % (h, t), [P, HALF], F32)
+            nc.scalar.activation(tanh_d[h, t][:], neg_diff, TANH, scale=-1.0)
+
+        def weigh_z(h, tag=""):
+            z_planes[h] = sbuf("z_planes%d" % h, [P, PACK, HALF], BF16, tag)
+            for t in range(PACK):
+                nc.vector.scalar_tensor_tensor(
+                    z_planes[h][:, t, :], tanh_d[h, t][:], gates[:, t : t + 1], a_bank[h, t], MULT, MULT
+                )
+
+        def group_z(h):
+            z_grouped[h] = sbuf("z_grouped%d" % h, [P, HALF, PACK], BF16)
+            interleave(nc.vector.tensor_copy, z_grouped[h][:], z_planes[h][:])
+
+        def moments(h):
+            codes, scales = quantize("z_half%d" % h, z_grouped[h], HALF)
+            for e in range(2):
+                r = 2 * h + e
+                cv_bank[r] = psum.tile([P, H], F32, name="cv_bank%d" % r, tag="bcv")
+                cols = slice(e * P, (e + 1) * P)
+                matmul(cv_bank[r][:], codes[:, cols], scales[:, cols], z2_codes[:], z2_scales[:])
+
+        def drain_cv(r):
+            cv_rows[r] = sbuf("cv_rows%d" % r, [P, H], F32)
+            nc.vector.tensor_scalar(cv_rows[r][:], cv_bank[r][:], 0.0625, None, MULT)
+
+        def squash_cv(r, src, scale):
+            neg_tanh[r] = sbuf("neg_tanh%d" % r, [P, H], F32)
+            nc.scalar.activation(neg_tanh[r][:], src[:], TANH, scale=scale)
+
+        def fetch_n3(r):
+            old[r] = sbuf("old%d" % r, [P, W], F32)
+            nc.scalar.activation(old[r][:], cv_rows[r][:].indirect(n3_list[:]), COPY)
+
+        def fetch_n4(r):
+            ra[r] = sbuf("ra%d" % r, [P, W], F32)
+            nc.vector.tensor_tensor(ra[r][:], neg_tanh[r][:].indirect(n4_list[:]), old[r][:], ADD)
+
+        def put_back(r):
+            nc.scalar.activation(cv_rows[r][:].indirect(n3_list[:]), ra[r][:], COPY)
+            nc.sync.dma_start(out[r * P : (r + 1) * P, :], cv_rows[r][:])
+
+        round_wa(0, "")
+        project_a(0)
         b_rows = [sbuf("b_rows%d" % t, [P, H], F32) for t in range(PACK)]
         z2_planes = sbuf("z2_planes", [P, PACK, H], BF16)
         for t in range(PACK):
-            nc.scalar.copy(b_rows[t][:], b_bank[t][:])
+            drain = nc.vector.tensor_copy if t == PACK - 1 else nc.scalar.copy
+            drain(b_rows[t][:], b_bank[t][:])
+        for t in range(PACK):
             nc.vector.tensor_scalar(z2_planes[:, t, :], b_rows[t][:], gates[:, PACK + t : PACK + t + 1], None, MULT)
-
-        a_bank, tanh_d, cv_bank, cv_rows, ra = {}, {}, {}, {}, {}
-        z2_mx = []
-
-        def project_a(ib):
-            grouped = sbuf("wa_grouped%d" % ib, [P, BLK, PACK], BF16)
-            interleave(nc.vector.tensor_copy, grouped[:], wa_raw[:, :, ib * BLK : (ib + 1) * BLK])
-            codes, scales = quantize("wa%d" % ib, grouped, BLK)
-            a_bank[ib] = psum.tile([P, PACK, BLK], F32, name="a_bank%d" % ib, tag="a")
-            for t in range(PACK):
-                matmul(a_bank[ib][:, t, :], xa_words[:, t, :], xa_scales[:, t, :], codes[:], scales[:])
-
-        def fetch_b(ib):
-            cols = slice(ib * LIST_COLS, (ib + 1) * LIST_COLS)
-            first = sbuf("b_n1_%d" % ib, [P, PACK, BLK], F32)
-            diff = sbuf("diff%d" % ib, [P, PACK, BLK], F32)
-            for t in range(PACK):
-                nc.scalar.activation(first[:, t, :], b_rows[t][:].indirect(n1_list[:, cols]), COPY)
-            for t in range(PACK):
-                nc.vector.tensor_tensor(diff[:, t, :], b_rows[t][:].indirect(n2_list[:, cols]), first[:, t, :], SUB)
-            tanh_d[ib] = sbuf("tanh_d%d" % ib, [P, PACK, BLK], F32)
-            nc.scalar.activation(tanh_d[ib][:], diff[:], TANH, scale=-1.0)
-
-        def make_z2():
-            grouped = sbuf("z2_grouped", [P, H, PACK], BF16)
-            interleave(nc.vector.tensor_copy, grouped[:], z2_planes[:])
-            z2_mx.extend(quantize("z2", grouped, H))
-
-        def moments(ib):
-            planes = sbuf("z_planes%d" % ib, [P, PACK, BLK], BF16)
-            for t in range(PACK):
-                nc.vector.scalar_tensor_tensor(
-                    planes[:, t, :], tanh_d[ib][:, t, :], gates[:, t : t + 1], a_bank[ib][:, t, :], MULT, MULT
-                )
-            grouped = sbuf("z_grouped%d" % ib, [P, BLK, PACK], BF16)
-            interleave(nc.vector.tensor_copy, grouped[:], planes[:])
-            codes, scales = quantize("z_block%d" % ib, grouped, BLK)
-            cv_bank[ib] = psum.tile([P, H], F32, name="cv_bank%d" % ib, tag="bcv")
-            matmul(cv_bank[ib][:], codes[:], scales[:], z2_mx[0][:], z2_mx[1][:])
-
-        def fetch_cv(ib):
-            cv_rows[ib] = sbuf("cv_rows%d" % ib, [P, H], F32)
-            nc.vector.tensor_scalar(cv_rows[ib][:], cv_bank[ib][:], 0.0625, None, MULT)
-            neg_tanh = sbuf("neg_tanh%d" % ib, [P, H], F32)
-            nc.scalar.activation(neg_tanh[:], cv_rows[ib][:], TANH, scale=-1.0)
-            old = sbuf("old%d" % ib, [P, W], F32)
-            nc.scalar.activation(old[:], cv_rows[ib][:].indirect(n3_list[:]), COPY)
-            ra[ib] = sbuf("ra%d" % ib, [P, W], F32)
-            nc.vector.tensor_tensor(ra[ib][:], neg_tanh[:].indirect(n4_list[:]), old[:], ADD)
-
-        def put_back(ib):
-            nc.scalar.activation(cv_rows[ib][:].indirect(n3_list[:]), ra[ib][:], COPY)
-            nc.sync.dma_start(out[ib * BLK : (ib + 1) * BLK, :], cv_rows[ib][:])
-
-        project_a(0)
-        fetch_b(0)
-        make_z2()
-        for ib in range(NBLK + 1):
-            if ib + 1 < NBLK:
-                project_a(ib + 1)
-                fetch_b(ib + 1)
-            if ib < NBLK:
-                moments(ib)
-                fetch_cv(ib)
-            if ib > 0:
-                put_back(ib - 1)
+        fetch_n1(0)
+        z2_grouped = sbuf("z2_grouped", [P, H, PACK], BF16)
+        cut = Z2_SCALAR_COLS
+        interleave(nc.vector.tensor_copy, z2_grouped[:, cut:, :], z2_planes[:, :, cut:])
+        interleave(nc.scalar.copy, z2_grouped[:, :cut, :], z2_planes[:, :, :cut])
+        neg_diff0 = sbuf("neg_diff0", [P, PACK, HALF], F32)
+        for t in range(PACK):
+            fetch_n2(0, t, neg_diff0[:, t, :])
+        z2_codes, z2_scales = quantize("z2", z2_grouped, H)
+        fetch_n1(1, "neg_diff0")
+        weigh_z(0)
+        group_z(0)
+        moments(0)
+        round_wa(1, "tanh_d03")
+        for r in (0, 1):
+            squash_cv(r, cv_bank[r], -0.0625)
+            drain_cv(r)
+        for r in (0, 1):
+            fetch_n3(r)
+        for t, tag in enumerate(("z_planes0", "z_grouped0", "z_half0_codes", "z_planes0")):
+            neg_diff1 = sbuf("neg_diff1%d" % t, [P, HALF], F32, tag)
+            fetch_n2(1, t, neg_diff1[:])
+        project_a(1, "z_half0_scales")
+        fetch_n4(0)
+        weigh_z(1, "old0")
+        fetch_n4(1)
+        group_z(1)
+        moments(1)
+        put_back(0)
+        put_back(1)
+        for r in (2, 3):
+            drain_cv(r)
+            squash_cv(r, cv_rows[r], -1.0)
+            fetch_n3(r)
+        for r in (2, 3):
+            fetch_n4(r)
+            put_back(r)

@@ -24,8 +24,8 @@ PACK = 4
 RUN = 8
 HALF = H // 2
 LIST_COLS = HALF // 16
-WB_SCALAR_COLS = (HALF, 160)
-Z2_SCALAR_COLS = 176
+WB_SCALAR_COLS = (144, 96)
+Z2_SCALAR_COLS = 320
 
 
 def interleave(copy, grouped, planes):
@@ -127,8 +127,7 @@ def tile_picked_momtjointbktanh_none_p_kernel(
             cut = WB_SCALAR_COLS[h]
             grouped = sbuf("wb_grouped%d" % h, [P, HALF, PACK], BF16)
             interleave(nc.scalar.copy, grouped[:, :cut, :], wb_raw[h][:, :, :cut])
-            if cut < HALF:
-                interleave(nc.vector.tensor_copy, grouped[:, cut:, :], wb_raw[h][:, :, cut:])
+            interleave(nc.vector.tensor_copy, grouped[:, cut:, :], wb_raw[h][:, :, cut:])
             codes, scales = quantize("wb%d" % h, grouped, HALF)
             for t in range(PACK):
                 matmul(b_bank[t][:, h * HALF : (h + 1) * HALF], xb_words[:, t, :], xb_scales[:, t, :], codes[:], scales[:])
@@ -141,9 +140,12 @@ def tile_picked_momtjointbktanh_none_p_kernel(
 
         wa_grouped, a_bank, b_n1, tanh_d, z_planes, z_grouped, cv_bank, cv_rows, neg_tanh, old, ra = ({} for i in range(11))
 
-        def round_wa(h, tag):
-            wa_grouped[h] = sbuf("wa_grouped%d" % h, [P, HALF, PACK], BF16, tag)
-            interleave(nc.scalar.copy, wa_grouped[h][:], wa_raw[h][:])
+        def round_on_gpsimd(dst, src):
+            nc.gpsimd.tensor_scalar(dst, src, 1.0, 0.0, MULT, ADD)
+
+        def round_wa(h):
+            wa_grouped[h] = sbuf("wa_grouped%d" % h, [P, HALF, PACK], BF16)
+            interleave(round_on_gpsimd, wa_grouped[h][:], wa_raw[h][:])
 
         def project_a(h, tag=""):
             codes, scales = quantize("wa%d" % h, wa_grouped[h], HALF, tag)
@@ -206,7 +208,8 @@ def tile_picked_momtjointbktanh_none_p_kernel(
             nc.scalar.activation(cv_rows[r][:].indirect(n3_list[:]), ra[r][:], COPY)
             nc.sync.dma_start(out[r * P : (r + 1) * P, :], cv_rows[r][:])
 
-        round_wa(0, "")
+        round_wa(0)
+        round_wa(1)
         project_a(0)
         b_rows = [sbuf("b_rows%d" % t, [P, H], F32) for t in range(PACK)]
         z2_planes = sbuf("z2_planes", [P, PACK, H], BF16)
@@ -228,11 +231,9 @@ def tile_picked_momtjointbktanh_none_p_kernel(
         weigh_z(0)
         group_z(0)
         moments(0)
-        round_wa(1, "tanh_d03")
         for r in (0, 1):
-            squash_cv(r, cv_bank[r], -0.0625)
             drain_cv(r)
-        for r in (0, 1):
+            squash_cv(r, cv_rows[r], -1.0)
             fetch_n3(r)
         for t, tag in enumerate(("z_planes0", "z_grouped0", "z_half0_codes", "z_planes0")):
             neg_diff1 = sbuf("neg_diff1%d" % t, [P, HALF], F32, tag)

from contextlib import ExitStack

import concourse.mybir as mybir
from concourse.masks import make_identity

K, T, S, H, W = 512, 2048, 512, 512, 384
FLOPS = 2 * K * S * H * 2 + 2 * S * H * H

F32 = mybir.dt.float32
BF16 = mybir.dt.bfloat16
I32 = mybir.dt.int32
U32 = mybir.dt.uint32
U16 = mybir.dt.uint16
U8 = mybir.dt.uint8
FP8X4 = mybir.dt.float8_e4m3fn_x4
MULT = mybir.AluOpType.mult
ADD = mybir.AluOpType.add
SUB = mybir.AluOpType.subtract
COPY = mybir.ActivationFunctionType.Copy
TANH = mybir.ActivationFunctionType.Tanh

P = 128
PACK = 4
RUN = 8
HALF = H // 2
LIST_COLS = HALF // 16
WB_SCALAR_COLS = (144, 96)
Z2_SCALAR_COLS = 320


def interleave(copy, grouped, planes):
    copy(
        grouped.rearrange("p (c i) t -> p c t i", i=4),
        planes.rearrange("p t (c i) -> p c t i", i=4),
    )


def tile_picked_momtjointbktanh_none_p_kernel(
    tc, x_words, x_scales, wa, wb, gt, gi, offs, two, n1, n2, n3, n4, out
):
    nc = tc.nc
    with ExitStack() as ctx:
        keep = ctx.enter_context(tc.tile_pool(name="keep", bufs=1))
        psum = ctx.enter_context(tc.psum_pool(name="psum", bufs=4))

        def sbuf(name, shape, dtype, tag=""):
            return keep.tile(shape, dtype, name=name, tag=tag, align_bytes=64)

        def load_list(name, src):
            dst = sbuf(name, list(src.shape), U16)
            nc.sync.dma_start(dst[:], src)
            return dst

        def load_weight_half(name, w, h):
            dst = sbuf("%s%d" % (name, h), [P, PACK, HALF], F32)
            nc.sync.dma_start(dst[:], w.rearrange("(p j) n -> p j n", j=PACK)[:, :, h * HALF : (h + 1) * HALF])
            return dst

        def quantize(name, grouped, width, tag=""):
            codes = sbuf(name + "_codes", [P, width], U32, tag)
            scales = sbuf(name + "_scales", [P, width], U8)
            nc.vector.quantize_mx(
                out=codes[:].bitcast(FP8X4), scales=scales[:], in_=grouped[:].rearrange("p n t -> p (n t)")
            )
            return codes, scales

        def matmul(dst, lhs_codes, lhs_scales, rhs_codes, rhs_scales):
            nc.tensor.matmul_mx(
                out=dst,
                lhsT=lhs_codes.bitcast(FP8X4),
                lhsT_scale=lhs_scales,
                rhs=rhs_codes.bitcast(FP8X4),
                rhs_scale=rhs_scales,
                start=True,
                stop=True,
            )

        scale_table = sbuf("scale_table", [P, T], U8)
        nc.gpsimd.memset(scale_table[:].bitcast(I32), 0)
        for q in range(4):
            nc.sync.dma_start(
                scale_table[32 * q : 32 * q + 4, :].bitcast(I32), x_scales[0, 4 * q : 4 * q + 4, :].bitcast(I32)
            )
        two_list = load_list("two_list", two)
        offs_list = load_list("offs_list", offs)
        word_table = sbuf("word_table", [P, T], I32)
        nc.sync.dma_start(word_table[:], x_words[0].rearrange("p n t -> p (n t)").bitcast(I32))
        wb_raw = [load_weight_half("wb_raw", wb, h) for h in range(2)]
        gate_rows = sbuf("gate_rows", [P, P], F32)
        nc.gpsimd.memset(gate_rows[:], 0.0)
        for row, gate in ((0, gt), (PACK, gi)):
            nc.sync.dma_start(
                gate_rows[row : row + PACK, :].rearrange("t (g r) -> t g r", r=RUN),
                gate.rearrange("(g t r) o -> t g (r o)", t=PACK, r=RUN),
            )
        identity = sbuf("identity", [P, P], F32)
        make_identity(nc, identity[:])
        n1_list = load_list("n1_list", n1)
        n2_list = load_list("n2_list", n2)
        wa_raw = [load_weight_half("wa_raw", wa, h) for h in range(2)]
        n3_list = load_list("n3_list", n3)
        n4_list = load_list("n4_list", n4)

        def pick_scales(name, entries):
            picked = sbuf(name + "_picked", [P, S], U8)
            nc.vector.tensor_copy(picked[:], scale_table[:].indirect(entries[:]))
            dealt = sbuf(name + "_dealt", [P, PACK, P], U8)
            nc.vector.tensor_copy(
                dealt[:].bitcast(I32).rearrange("p t (g w) -> p g t w", w=RUN // 4),
                picked[:].bitcast(I32).rearrange("p (g t w) -> p g t w", t=PACK, w=RUN // 4),
            )
            return dealt

        def pick_words(name, entries, tag=""):
            dealt = sbuf(name, [P, PACK, P], U32, tag)
            nc.vector.tensor_copy(
                dealt[:].rearrange("p t (g r) -> p g t r", r=RUN), word_table[:].bitcast(U32).indirect(entries[:])
            )
            return dealt

        xb_scales = pick_scales("xb_scales", two_list)
        xa_scales = pick_scales("xa_scales", offs_list)
        xb_words = pick_words("xb_words", two_list)

        b_bank = [psum.tile([P, H], F32, name="b_bank%d" % t, tag="bcv") for t in range(PACK)]
        for h in range(2):
            cut = WB_SCALAR_COLS[h]
            grouped = sbuf("wb_grouped%d" % h, [P, HALF, PACK], BF16)
            interleave(nc.scalar.copy, grouped[:, :cut, :], wb_raw[h][:, :, :cut])
            interleave(nc.vector.tensor_copy, grouped[:, cut:, :], wb_raw[h][:, :, cut:])
            codes, scales = quantize("wb%d" % h, grouped, HALF)
            for t in range(PACK):
                matmul(b_bank[t][:, h * HALF : (h + 1) * HALF], xb_words[:, t, :], xb_scales[:, t, :], codes[:], scales[:])

        xa_words = pick_words("xa_words", offs_list, "wb_grouped1")
        gate_bank = psum.tile([P, P], F32, name="gate_bank", tag="a")
        nc.tensor.transpose(gate_bank[:], gate_rows[:], identity[:])
        gates = sbuf("gates", [P, 2 * PACK], F32)
        nc.scalar.copy(gates[:], gate_bank[:, 0 : 2 * PACK])

        wa_grouped, a_bank, b_n1, tanh_d, z_planes, z_grouped, cv_bank, cv_rows, neg_tanh, old, ra = ({} for i in range(11))

        def round_on_gpsimd(dst, src):
            nc.gpsimd.tensor_scalar(dst, src, 1.0, 0.0, MULT, ADD)

        def round_wa(h):
            wa_grouped[h] = sbuf("wa_grouped%d" % h, [P, HALF, PACK], BF16)
            interleave(round_on_gpsimd, wa_grouped[h][:], wa_raw[h][:])

        def project_a(h, tag=""):
            codes, scales = quantize("wa%d" % h, wa_grouped[h], HALF, tag)
            for u in range(2):
                bank = psum.tile([P, 2, HALF], F32, name="a_bank%d%d" % (h, u), tag="a")
                for e in range(2):
                    t = 2 * u + e
                    a_bank[h, t] = bank[:, e, :]
                    matmul(a_bank[h, t], xa_words[:, t, :], xa_scales[:, t, :], codes[:], scales[:])

        def entries(lst, h):
            return lst[:, h * LIST_COLS : (h + 1) * LIST_COLS]

        def fetch_n1(h, tag=""):
            b_n1[h] = sbuf("b_n1_%d" % h, [P, PACK, HALF], F32, tag)
            for t in range(PACK):
                nc.scalar.activation(b_n1[h][:, t, :], b_rows[t][:].indirect(entries(n1_list, h)), COPY)

        def fetch_n2(h, t, neg_diff):
            nc.vector.tensor_tensor(neg_diff, b_rows[t][:].indirect(entries(n2_list, h)), b_n1[h][:, t, :], SUB)
            tanh_d[h, t] = sbuf("tanh_d%d%d" % (h, t), [P, HALF], F32)
            nc.scalar.activation(tanh_d[h, t][:], neg_diff, TANH, scale=-1.0)

        def weigh_z(h, tag=""):
            z_planes[h] = sbuf("z_planes%d" % h, [P, PACK, HALF], BF16, tag)
            for t in range(PACK):
                nc.vector.scalar_tensor_tensor(
                    z_planes[h][:, t, :], tanh_d[h, t][:], gates[:, t : t + 1], a_bank[h, t], MULT, MULT
                )

        def group_z(h):
            z_grouped[h] = sbuf("z_grouped%d" % h, [P, HALF, PACK], BF16)
            interleave(nc.vector.tensor_copy, z_grouped[h][:], z_planes[h][:])

        def moments(h):
            codes, scales = quantize("z_half%d" % h, z_grouped[h], HALF)
            for e in range(2):
                r = 2 * h + e
                cv_bank[r] = psum.tile([P, H], F32, name="cv_bank%d" % r, tag="bcv")
                cols = slice(e * P, (e + 1) * P)
                matmul(cv_bank[r][:], codes[:, cols], scales[:, cols], z2_codes[:], z2_scales[:])

        def drain_cv(r):
            cv_rows[r] = sbuf("cv_rows%d" % r, [P, H], F32)
            nc.vector.tensor_scalar(cv_rows[r][:], cv_bank[r][:], 0.0625, None, MULT)

        def squash_cv(r, src, scale):
            neg_tanh[r] = sbuf("neg_tanh%d" % r, [P, H], F32)
            nc.scalar.activation(neg_tanh[r][:], src[:], TANH, scale=scale)

        def fetch_n3(r):
            old[r] = sbuf("old%d" % r, [P, W], F32)
            nc.scalar.activation(old[r][:], cv_rows[r][:].indirect(n3_list[:]), COPY)

        def fetch_n4(r):
            ra[r] = sbuf("ra%d" % r, [P, W], F32)
            nc.vector.tensor_tensor(ra[r][:], neg_tanh[r][:].indirect(n4_list[:]), old[r][:], ADD)

        def put_back(r):
            nc.scalar.activation(cv_rows[r][:].indirect(n3_list[:]), ra[r][:], COPY)
            nc.sync.dma_start(out[r * P : (r + 1) * P, :], cv_rows[r][:])

        round_wa(0)
        round_wa(1)
        project_a(0)
        b_rows = [sbuf("b_rows%d" % t, [P, H], F32) for t in range(PACK)]
        z2_planes = sbuf("z2_planes", [P, PACK, H], BF16)
        for t in range(PACK):
            drain = nc.vector.tensor_copy if t == PACK - 1 else nc.scalar.copy
            drain(b_rows[t][:], b_bank[t][:])
        for t in range(PACK):
            nc.vector.tensor_scalar(z2_planes[:, t, :], b_rows[t][:], gates[:, PACK + t : PACK + t + 1], None, MULT)
        fetch_n1(0)
        z2_grouped = sbuf("z2_grouped", [P, H, PACK], BF16)
        cut = Z2_SCALAR_COLS
        interleave(nc.vector.tensor_copy, z2_grouped[:, cut:, :], z2_planes[:, :, cut:])
        interleave(nc.scalar.copy, z2_grouped[:, :cut, :], z2_planes[:, :, :cut])
        neg_diff0 = sbuf("neg_diff0", [P, PACK, HALF], F32)
        for t in range(PACK):
            fetch_n2(0, t, neg_diff0[:, t, :])
        z2_codes, z2_scales = quantize("z2", z2_grouped, H)
        fetch_n1(1, "neg_diff0")
        weigh_z(0)
        group_z(0)
        moments(0)
        for r in (0, 1):
            drain_cv(r)
            squash_cv(r, cv_rows[r], -1.0)
            fetch_n3(r)
        for t, tag in enumerate(("z_planes0", "z_grouped0", "z_half0_codes", "z_planes0")):
            neg_diff1 = sbuf("neg_diff1%d" % t, [P, HALF], F32, tag)
            fetch_n2(1, t, neg_diff1[:])
        project_a(1, "z_half0_scales")
        fetch_n4(0)
        weigh_z(1, "old0")
        fetch_n4(1)
        group_z(1)
        moments(1)
        put_back(0)
        put_back(1)
        for r in (2, 3):
            drain_cv(r)
            squash_cv(r, cv_rows[r], -1.0)
            fetch_n3(r)
        for r in (2, 3):
            fetch_n4(r)
            put_back(r)
